import numpy as np
import ml_dtypes


def mxq(x, axis, fmt="e4m3"):
    dtype, down = {"e4m3": (ml_dtypes.float8_e4m3fn, 7), "e5m2": (ml_dtypes.float8_e5m2, 14)}[fmt]
    v = np.moveaxis(np.asarray(x, np.float32).astype(ml_dtypes.bfloat16).astype(np.float64), axis, -1)
    blocks = v.reshape(v.shape[:-1] + (-1, 32))
    amax = np.abs(blocks).max(-1, keepdims=True)
    byte = np.maximum(np.where(amax > 0, np.frexp(amax)[1] - 1 + 127, 0) - down, 1)
    scale = np.exp2(byte - 127.0)
    codes = (blocks / scale).astype(np.float32).astype(dtype).astype(np.float64)
    return np.moveaxis((codes * scale).reshape(v.shape), -1, axis)


WIDE = False


def mx_kscale(k):
    if not WIDE:
        return np.ones(k)
    levels = np.array([10, -10, 5, -5, 0])
    if k % 512:
        return np.exp2(np.random.permutation(np.resize(levels, k // 32))).repeat(32)
    a = np.empty((k // 512, 16))
    for p in range(k // 512):
        a[p, :8] = np.random.permutation(np.resize(levels, 8))
        for g in range(8):
            far = levels[np.abs(levels - a[p, g]) >= 10]
            a[p, g + 8] = far[np.random.randint(len(far))]
    return np.exp2(a.ravel()).repeat(32)


def f64(x):
    return np.asarray(x).astype(np.float64)


def striped8(idx):
    return np.concatenate([v.reshape(-1, 16).T for v in idx]).astype(np.uint16)


def unstriped8(offs):
    return np.stack([offs[16 * g:16 * g + 16].T.reshape(-1) for g in range(8)]).astype(np.int64)


E2M1 = np.array([0.0, 0.5, 1.0, 1.5, 2.0, 3.0, 4.0, 6.0, -0.0, -0.5, -1.0, -1.5, -2.0, -3.0, -4.0, -6.0])


def pack_weight(w, fmt):
    k, n = w.shape
    w = f64(np.asarray(w, np.float32).astype(ml_dtypes.bfloat16)).reshape(k // 32, 32, n)
    amax = np.abs(w).max(1)
    if fmt == "e4m3":
        byte = np.frexp(amax)[1] - 1 + 127 - 7
    else:
        mant, ex = np.frexp(amax / 6.0)
        byte = np.where(mant > 0.5, ex, ex - 1) + 127
    byte = np.clip(np.where(amax > 0, byte, 1), 1, 254)
    scaled = (w * np.exp2(127.0 - byte)[:, None, :]).reshape(k, n).astype(np.float32)
    by_word = np.ascontiguousarray(scaled.reshape(k // 512, 128, 4, n).transpose(0, 1, 3, 2))
    if fmt == "e4m3":
        words = by_word.astype(ml_dtypes.float8_e4m3fn).view(np.uint8)
    else:
        c = by_word.astype(ml_dtypes.float4_e2m1fn).view(np.uint8) & 0xF
        words = (c[..., 0::2] | (c[..., 1::2] << 4)).reshape(k // 512, 128, 2 * n)
    return np.ascontiguousarray(words), np.ascontiguousarray(byte.astype(np.uint8).reshape(k // 512, 16, n))


def unpack_weight(words, scales, fmt):
    g, _, n = scales.shape
    words = np.ascontiguousarray(words).reshape(g, 128, n, -1)
    if fmt == "e4m3":
        vals = words.view(ml_dtypes.float8_e4m3fn).astype(np.float64)
    else:
        nib = np.empty((g, 128, n, 4), np.uint8)
        nib[..., 0::2] = words & 0xF
        nib[..., 1::2] = words >> 4
        vals = E2M1[nib]
    vals = vals * np.repeat(np.exp2(scales.astype(np.float64) - 127.0), 8, axis=1)[..., None]
    return vals.transpose(0, 1, 3, 2).reshape(g * 512, n)


def silu(v):
    return v / (1.0 + np.exp(-np.maximum(v, -700.0)))


K, M, T, S = 1536, 256, 1024, 512


def setup_inputs():
    n = np.random.standard_normal
    s = mx_kscale(K)[:, None]
    p_w = pack_weight(n((K, M)) / np.sqrt(K) / s, "e4m3")
    return {
        "xT": (n((K, T)) * s).astype(np.float32),
        "w_words": p_w[0],
        "w_scales": p_w[1],
        "wgt": np.repeat(np.random.uniform(0.5, 2.0, (8, S)), 16, axis=0).astype(np.float32),
        "b": (0.3 * n(256)).astype(np.float32),
        "wgo": np.repeat(np.random.uniform(0.5, 2.0, (8, S)), 16, axis=0).astype(np.float32),
        "offs": striped8(np.stack([np.random.permutation(T)[:S] for _ in range(8)])),
        "offs2": striped8(np.stack([np.random.permutation(T)[:S] for _ in range(8)])),
    }


def reference(xT, w_words, w_scales, wgt, b, wgo, offs, offs2):
    idx = unstriped8(offs)
    group = np.arange(K) % 512 // 64
    xg = f64(wgt)[np.arange(K) // 4 % 128] * f64(xT)[np.arange(K)[:, None], idx[group]]
    xT_ = mxq(xg, 0, "e4m3")
    w_ = unpack_weight(w_words, w_scales, "e4m3")
    y = w_.T @ xT_
    place = unstriped8(offs2)[np.arange(M) % 128 // 16]
    out = np.zeros((M, T))
    out[np.arange(M)[:, None], place] = f64(wgo)[np.arange(M) % 128] * (silu(y + f64(b)[:, None]))
    return out

@@ -1,0 +1,203 @@
+from contextlib import ExitStack
+
+import concourse.mybir as mybir
+
+FLOPS = 2 * 1536 * 256 * 512
+
+F32 = mybir.dt.float32
+BF16 = mybir.dt.bfloat16
+I32 = mybir.dt.int32
+U32 = mybir.dt.uint32
+U16 = mybir.dt.uint16
+U8 = mybir.dt.uint8
+FP8X4 = mybir.dt.float8_e4m3fn_x4
+MULT = mybir.AluOpType.mult
+COPY = mybir.ActivationFunctionType.Copy
+SILU = mybir.ActivationFunctionType.Silu
+
+P = 128
+PACK = 4
+PASSES = 3
+TOKENS = 1024
+PICKS = 512
+HALF = 256
+HCOLS = HALF // 16
+M_TILES = 2
+
+
+def tile_list_hboth_silu_kernel(tc, xT, w_words, w_scales, wgt, b, wgo, offs, offs2, out):
+    nc = tc.nc
+    with ExitStack() as ctx:
+        lists = ctx.enter_context(tc.tile_pool(name="lists", bufs=1))
+        keep = ctx.enter_context(tc.tile_pool(name="keep", bufs=1))
+        psum = ctx.enter_context(tc.psum_pool(name="psum", bufs=1))
+
+        offs_t = lists.tile([P, PICKS // 16], U16, name="offs_t")
+        offs2_t = lists.tile([P, PICKS // 16], U16, name="offs2_t")
+        wsc = keep.tile([P, PASSES * 256], U8, name="wsc", align_bytes=64)
+        ww = keep.tile([P, PASSES * 256], I32, name="ww", align_bytes=64)
+        bias = keep.tile([P, M_TILES], F32, name="bias")
+        warm = keep.tile([P, 1], F32, name="warm")
+        wgo_t = keep.tile([P, PICKS], F32, name="wgo_t")
+        wgt_t = [keep.tile([P, HALF], F32, name=f"wgt{h}") for h in range(2)]
+        win = [keep.tile([P, TOKENS], F32, name=f"win{m}") for m in range(M_TILES)]
+        x = {}
+        for a in range(PASSES):
+            for t in range(PACK):
+                x[a, t] = keep.tile([P, TOKENS], F32, name=f"x{a}{t}")
+
+        nc.vector.memset(wsc[:].bitcast(I32), 0)
+        nc.gpsimd.memset(warm[:], 0.0)
+        for m in range(M_TILES):
+            nc.gpsimd.memset(win[m][:], 0.0)
+        nc.scalar.activation(warm[:], warm[:], SILU)
+
+        planes = xT.rearrange("(a p t) n -> a t p n", p=P, t=PACK)
+        scale_rows = w_scales.rearrange("a (q r) n -> r q a n", r=PACK)
+
+        def load_x(a, t):
+            nc.sync.dma_start(x[a, t][:], planes[a, t])
+
+        nc.sync.dma_start(offs_t[:], offs)
+        load_x(0, 0)
+        nc.sync.dma_start(wgt_t[0][:], wgt[:, 0:HALF])
+        nc.sync.dma_start(wgt_t[1][:], wgt[:, HALF:PICKS])
+        load_x(0, 1)
+        load_x(0, 2)
+        load_x(0, 3)
+        load_x(1, 0)
+        load_x(1, 1)
+        load_x(1, 2)
+        load_x(1, 3)
+        for r in range(PACK):
+            nc.sync.dma_start(
+                wsc[:].bitcast(I32)[r:P:32, :].rearrange("q (a n) -> q a n", a=PASSES),
+                scale_rows[r].bitcast(I32),
+            )
+        with nc.allow_non_contiguous_dma(reason="one bias value to a partition"):
+            nc.sync.dma_start(bias[:], b.rearrange("(m p) -> p m", p=P))
+        load_x(2, 0)
+        load_x(2, 1)
+        load_x(2, 2)
+        load_x(2, 3)
+        nc.sync.dma_start(
+            ww[:].rearrange("p (a n) -> p a n", a=PASSES),
+            w_words.rearrange("a p n i -> p a (n i)").bitcast(I32),
+        )
+        nc.sync.dma_start(offs2_t[:], offs2)
+        nc.sync.dma_start(wgo_t[:], wgo)
+
+        pieces = {0: [(0, 512)], 1: [(0, 256), (256, 256)], 2: [(0, 256), (256, 128), (384, 128)]}
+        g4 = {}
+        grouped = {}
+        codes = {}
+        scales = {}
+        for a in range(PASSES):
+            for s, n in pieces[a]:
+                g4[a, s] = keep.tile([P, PACK, n], F32, name=f"g{a}_{s}")
+                grouped[a, s] = keep.tile([P, n, PACK], BF16, name=f"r{a}_{s}", align_bytes=64)
+            codes[a] = keep.tile([P, PICKS], U32, name=f"c{a}", align_bytes=64)
+            scales[a] = keep.tile([P, PICKS], U8, name=f"s{a}", align_bytes=64)
+        acc = {}
+        for m in range(M_TILES):
+            for h in range(2):
+                acc[m, h] = psum.tile([P, HALF], F32, name=f"acc{m}{h}")
+
+        def gather(a, t, s, n):
+            p0, pn = [(q, w) for q, w in pieces[a] if q <= s < q + w][0]
+            h = s // HALF
+            nc.vector.tensor_tensor(
+                g4[a, p0][:, t, s - p0 : s - p0 + n],
+                x[a, t][:].indirect(offs_t[:, s // 16 : (s + n) // 16]),
+                wgt_t[h][:, s - h * HALF : s - h * HALF + n],
+                MULT,
+            )
+
+        def interleave(a, s):
+            nc.scalar.copy(grouped[a, s][:], g4[a, s][:].rearrange("p t n -> p n t"))
+
+        def quantize(a, s):
+            n = dict(pieces[a])[s]
+            nc.vector.quantize_mx(
+                out=codes[a][:, s : s + n].bitcast(FP8X4),
+                scales=scales[a][:, s : s + n],
+                in_=grouped[a, s][:].rearrange("p n t -> p (n t)"),
+            )
+
+        def multiply(a, h):
+            for m in range(M_TILES):
+                cols = slice(a * 256 + m * P, a * 256 + (m + 1) * P)
+                picks = slice(h * HALF, (h + 1) * HALF)
+                nc.tensor.matmul_mx(
+                    out=acc[m, h][:],
+                    lhsT=ww[:, cols].bitcast(FP8X4),
+                    lhsT_scale=wsc[:, cols],
+                    rhs=codes[a][:, picks].bitcast(FP8X4),
+                    rhs_scale=scales[a][:, picks],
+                    start=(a == 0),
+                    stop=(a == PASSES - 1),
+                )
+
+        y = {}
+
+        def act(m, h):
+            y[m, h] = keep.tile([P, HALF], F32, name=f"y{m}{h}")
+            nc.scalar.activation(y[m, h][:], acc[m, h][:], SILU, bias=bias[:, m : m + 1])
+
+        def scatter(m, h):
+            nc.vector.tensor_tensor(
+                win[m][:].indirect(offs2_t[:, h * HCOLS : (h + 1) * HCOLS]),
+                y[m, h][:],
+                wgo_t[:, h * HALF : (h + 1) * HALF],
+                MULT,
+            )
+
+        for t in range(PACK):
+            gather(0, t, 0, 256)
+            gather(0, t, 256, 256)
+        interleave(0, 0)
+        for t in range(PACK):
+            gather(1, t, 0, 256)
+            if t < 2:
+                gather(1, t, 256, 256)
+            if t == 2:
+                quantize(0, 0)
+                multiply(0, 0)
+                multiply(0, 1)
+        interleave(1, 0)
+        for t in range(PACK):
+            gather(2, t, 0, 256)
+            if t == 2:
+                quantize(1, 0)
+                multiply(1, 0)
+        interleave(2, 0)
+        gather(1, 2, 256, 256)
+        gather(1, 3, 256, 256)
+        interleave(1, 256)
+        gather(2, 0, 256, 128)
+        gather(2, 1, 256, 128)
+        quantize(2, 0)
+        multiply(2, 0)
+        act(0, 0)
+        act(1, 0)
+        gather(2, 2, 256, 128)
+        gather(2, 3, 256, 128)
+        interleave(2, 256)
+        gather(2, 0, 384, 128)
+        quantize(1, 256)
+        multiply(1, 1)
+        gather(2, 1, 384, 128)
+        gather(2, 2, 384, 128)
+        gather(2, 3, 384, 128)
+        interleave(2, 384)
+        quantize(2, 256)
+        scatter(0, 0)
+        quantize(2, 384)
+        multiply(2, 1)
+        scatter(1, 0)
+        act(0, 1)
+        act(1, 1)
+        scatter(0, 1)
+        nc.sync.dma_start(out[0:P, :], win[0][:])
+        scatter(1, 1)
+        nc.sync.dma_start(out[P : 2 * P, :], win[1][:])

@@ -39,7 +39,7 @@ def tile_list_hboth_silu_kernel(tc, xT, w_words, w_scales, wgt, b, wgo, offs, of
         bias = keep.tile([P, M_TILES], F32, name="bias")
         warm = keep.tile([P, 1], F32, name="warm")
         wgo_t = keep.tile([P, PICKS], F32, name="wgo_t")
-        wgt_t = [keep.tile([P, HALF], F32, name=f"wgt{h}") for h in range(2)]
+        wgt_t = {0: keep.tile([P, 128], F32, name="wgt_0"), 128: keep.tile([P, 384], F32, name="wgt_128")}
         win = [keep.tile([P, TOKENS], F32, name=f"win{m}") for m in range(M_TILES)]
         x = {}
         for a in range(PASSES):
@@ -49,7 +49,7 @@ def tile_list_hboth_silu_kernel(tc, xT, w_words, w_scales, wgt, b, wgo, offs, of
         nc.vector.memset(wsc[:].bitcast(I32), 0)
         nc.gpsimd.memset(warm[:], 0.0)
         for m in range(M_TILES):
-            nc.gpsimd.memset(win[m][:], 0.0)
+            nc.vector.memset(win[m][:], 0.0)
         nc.scalar.activation(warm[:], warm[:], SILU)
 
         planes = xT.rearrange("(a p t) n -> a t p n", p=P, t=PACK)
@@ -58,10 +58,16 @@ def tile_list_hboth_silu_kernel(tc, xT, w_words, w_scales, wgt, b, wgo, offs, of
         def load_x(a, t):
             nc.sync.dma_start(x[a, t][:], planes[a, t])
 
+        def load_scales(r):
+            nc.sync.dma_start(
+                wsc[:].bitcast(I32)[r:P:32, :].rearrange("q (a n) -> q a n", a=PASSES),
+                scale_rows[r].bitcast(I32),
+            )
+
         nc.sync.dma_start(offs_t[:], offs)
+        nc.sync.dma_start(wgt_t[0][:], wgt[:, 0:128])
         load_x(0, 0)
-        nc.sync.dma_start(wgt_t[0][:], wgt[:, 0:HALF])
-        nc.sync.dma_start(wgt_t[1][:], wgt[:, HALF:PICKS])
+        nc.sync.dma_start(wgt_t[128][:], wgt[:, 128:512])
         load_x(0, 1)
         load_x(0, 2)
         load_x(0, 3)
@@ -69,13 +75,6 @@ def tile_list_hboth_silu_kernel(tc, xT, w_words, w_scales, wgt, b, wgo, offs, of
         load_x(1, 1)
         load_x(1, 2)
         load_x(1, 3)
-        for r in range(PACK):
-            nc.sync.dma_start(
-                wsc[:].bitcast(I32)[r:P:32, :].rearrange("q (a n) -> q a n", a=PASSES),
-                scale_rows[r].bitcast(I32),
-            )
-        with nc.allow_non_contiguous_dma(reason="one bias value to a partition"):
-            nc.sync.dma_start(bias[:], b.rearrange("(m p) -> p m", p=P))
         load_x(2, 0)
         load_x(2, 1)
         load_x(2, 2)
@@ -84,17 +83,23 @@ def tile_list_hboth_silu_kernel(tc, xT, w_words, w_scales, wgt, b, wgo, offs, of
             ww[:].rearrange("p (a n) -> p a n", a=PASSES),
             w_words.rearrange("a p n i -> p a (n i)").bitcast(I32),
         )
+        for r in range(PACK):
+            load_scales(r)
+        with nc.allow_non_contiguous_dma(reason="one bias value to a partition"):
+            nc.sync.dma_start(bias[:], b.rearrange("(m p) -> p m", p=P))
         nc.sync.dma_start(offs2_t[:], offs2)
         nc.sync.dma_start(wgo_t[:], wgo)
 
-        pieces = {0: [(0, 512)], 1: [(0, 256), (256, 256)], 2: [(0, 256), (256, 128), (384, 128)]}
+        pieces = {0: 128, 128: 384}
+        qpieces = {0: [(0, 512)], 1: [(0, 256), (256, 256)], 2: [(0, 128), (128, 128), (256, 256)]}
         g4 = {}
         grouped = {}
         codes = {}
         scales = {}
         for a in range(PASSES):
-            for s, n in pieces[a]:
+            for s, n in pieces.items():
                 g4[a, s] = keep.tile([P, PACK, n], F32, name=f"g{a}_{s}")
+            for s, n in qpieces[a]:
                 grouped[a, s] = keep.tile([P, n, PACK], BF16, name=f"r{a}_{s}", align_bytes=64)
             codes[a] = keep.tile([P, PICKS], U32, name=f"c{a}", align_bytes=64)
             scales[a] = keep.tile([P, PICKS], U8, name=f"s{a}", align_bytes=64)
@@ -103,21 +108,25 @@ def tile_list_hboth_silu_kernel(tc, xT, w_words, w_scales, wgt, b, wgo, offs, of
             for h in range(2):
                 acc[m, h] = psum.tile([P, HALF], F32, name=f"acc{m}{h}")
 
-        def gather(a, t, s, n):
-            p0, pn = [(q, w) for q, w in pieces[a] if q <= s < q + w][0]
-            h = s // HALF
+        def gather(a, t, s):
+            n = pieces[s]
             nc.vector.tensor_tensor(
-                g4[a, p0][:, t, s - p0 : s - p0 + n],
+                g4[a, s][:, t, :],
                 x[a, t][:].indirect(offs_t[:, s // 16 : (s + n) // 16]),
-                wgt_t[h][:, s - h * HALF : s - h * HALF + n],
+                wgt_t[s][:],
                 MULT,
             )
 
-        def interleave(a, s):
-            nc.scalar.copy(grouped[a, s][:], g4[a, s][:].rearrange("p t n -> p n t"))
+        def interleave(a, s, n):
+            q0 = [q for q, w in qpieces[a] if q <= s < q + w][0]
+            g0 = 0 if s < 128 else 128
+            nc.scalar.copy(
+                grouped[a, q0][:, s - q0 : s - q0 + n, :],
+                g4[a, g0][:, :, s - g0 : s - g0 + n].rearrange("p t n -> p n t"),
+            )
 
         def quantize(a, s):
-            n = dict(pieces[a])[s]
+            n = dict(qpieces[a])[s]
             nc.vector.quantize_mx(
                 out=codes[a][:, s : s + n].bitcast(FP8X4),
                 scales=scales[a][:, s : s + n],
@@ -153,51 +162,47 @@ def tile_list_hboth_silu_kernel(tc, xT, w_words, w_scales, wgt, b, wgo, offs, of
             )
 
         for t in range(PACK):
-            gather(0, t, 0, 256)
-            gather(0, t, 256, 256)
-        interleave(0, 0)
+            if t == 0:
+                gather(0, t, 0)
+            gather(0, t, 128)
+        interleave(0, 128, 384)
         for t in range(PACK):
-            gather(1, t, 0, 256)
-            if t < 2:
-                gather(1, t, 256, 256)
+            gather(1, t, 128)
+        for t in range(1, PACK):
+            gather(0, t, 0)
+        interleave(0, 0, 128)
+        interleave(1, 256, 256)
+        interleave(1, 128, 128)
+        for t in range(PACK):
+            gather(2, t, 128)
             if t == 2:
                 quantize(0, 0)
                 multiply(0, 0)
                 multiply(0, 1)
-        interleave(1, 0)
+                quantize(1, 256)
+                multiply(1, 1)
+        interleave(2, 256, 256)
+        interleave(2, 128, 128)
         for t in range(PACK):
-            gather(2, t, 0, 256)
-            if t == 2:
-                quantize(1, 0)
-                multiply(1, 0)
-        interleave(2, 0)
-        gather(1, 2, 256, 256)
-        gather(1, 3, 256, 256)
-        interleave(1, 256)
-        gather(2, 0, 256, 128)
-        gather(2, 1, 256, 128)
-        quantize(2, 0)
-        multiply(2, 0)
-        act(0, 0)
-        act(1, 0)
-        gather(2, 2, 256, 128)
-        gather(2, 3, 256, 128)
-        interleave(2, 256)
-        gather(2, 0, 384, 128)
-        quantize(1, 256)
-        multiply(1, 1)
-        gather(2, 1, 384, 128)
-        gather(2, 2, 384, 128)
-        gather(2, 3, 384, 128)
-        interleave(2, 384)
+            gather(1, t, 0)
+        interleave(1, 0, 128)
         quantize(2, 256)
-        scatter(0, 0)
-        quantize(2, 384)
         multiply(2, 1)
-        scatter(1, 0)
         act(0, 1)
         act(1, 1)
+        for t in range(PACK):
+            gather(2, t, 0)
+        interleave(2, 0, 128)
+        quantize(2, 128)
+        quantize(1, 0)
+        multiply(1, 0)
         scatter(0, 1)
-        nc.sync.dma_start(out[0:P, :], win[0][:])
+        quantize(2, 0)
+        multiply(2, 0)
         scatter(1, 1)
+        act(0, 0)
+        act(1, 0)
+        scatter(0, 0)
+        nc.sync.dma_start(out[0:P, :], win[0][:])
+        scatter(1, 0)
         nc.sync.dma_start(out[P : 2 * P, :], win[1][:])

@@ -2,8 +2,6 @@ from contextlib import ExitStack
 
 import concourse.mybir as mybir
 
-FLOPS = 2 * 1536 * 256 * 512
-
 F32 = mybir.dt.float32
 BF16 = mybir.dt.bfloat16
 I32 = mybir.dt.int32
@@ -12,17 +10,24 @@ U16 = mybir.dt.uint16
 U8 = mybir.dt.uint8
 FP8X4 = mybir.dt.float8_e4m3fn_x4
 MULT = mybir.AluOpType.mult
-COPY = mybir.ActivationFunctionType.Copy
 SILU = mybir.ActivationFunctionType.Silu
 
 P = 128
 PACK = 4
-PASSES = 3
+K = 1536
+PASSES = K // (P * PACK)
+ROWS = 256
+ROW_TILES = ROWS // P
 TOKENS = 1024
 PICKS = 512
-HALF = 256
-HCOLS = HALF // 16
-M_TILES = 2
+HALF = PICKS // 2
+LIST_STRIPE = 16
+
+NARROW = 0
+WIDE = 128
+PIECE_PICKS = {NARROW: 128, WIDE: 384}
+
+FLOPS = 2 * K * ROWS * PICKS
 
 
 def tile_list_hboth_silu_kernel(tc, xT, w_words, w_scales, wgt, b, wgo, offs, offs2, out):
@@ -32,177 +37,153 @@ def tile_list_hboth_silu_kernel(tc, xT, w_words, w_scales, wgt, b, wgo, offs, of
         keep = ctx.enter_context(tc.tile_pool(name="keep", bufs=1))
         psum = ctx.enter_context(tc.psum_pool(name="psum", bufs=1))
 
-        offs_t = lists.tile([P, PICKS // 16], U16, name="offs_t")
-        offs2_t = lists.tile([P, PICKS // 16], U16, name="offs2_t")
-        wsc = keep.tile([P, PASSES * 256], U8, name="wsc", align_bytes=64)
-        ww = keep.tile([P, PASSES * 256], I32, name="ww", align_bytes=64)
-        bias = keep.tile([P, M_TILES], F32, name="bias")
-        warm = keep.tile([P, 1], F32, name="warm")
-        wgo_t = keep.tile([P, PICKS], F32, name="wgo_t")
-        wgt_t = {0: keep.tile([P, 128], F32, name="wgt_0"), 128: keep.tile([P, 384], F32, name="wgt_128")}
-        win = [keep.tile([P, TOKENS], F32, name=f"win{m}") for m in range(M_TILES)]
-        x = {}
+        gather_list = lists.tile([P, PICKS // LIST_STRIPE], U16, name="gather_list")
+        scatter_list = lists.tile([P, PICKS // LIST_STRIPE], U16, name="scatter_list")
+        weight_scales = keep.tile([P, PASSES * ROWS], U8, name="weight_scales", align_bytes=64)
+        weight_codes = keep.tile([P, PASSES * ROWS], I32, name="weight_codes", align_bytes=64)
+        bias = keep.tile([P, ROW_TILES], F32, name="bias")
+        silu_input = keep.tile([P, 1], F32, name="silu_input")
+        wgo_tile = keep.tile([P, PICKS], F32, name="wgo_tile")
+        wgt_narrow = keep.tile([P, PIECE_PICKS[NARROW]], F32, name="wgt_narrow")
+        wgt_wide = keep.tile([P, PIECE_PICKS[WIDE]], F32, name="wgt_wide", tag="wgt_wide")
+        wgt_tiles = {NARROW: wgt_narrow, WIDE: wgt_wide}
+        windows = [keep.tile([P, TOKENS], F32, name=f"window_{m}") for m in range(ROW_TILES)]
+        tables = {
+            (a, i): keep.tile([P, TOKENS], F32, name=f"table_{a}_{i}") for a in range(PASSES) for i in range(PACK)
+        }
+
+        nc.vector.memset(weight_scales[:].bitcast(I32), 0)
+        for m in range(ROW_TILES):
+            nc.vector.memset(windows[m][:], 0.0)
+        nc.gpsimd.memset(silu_input[:], 0.0)
+        nc.scalar.activation(silu_input[:], silu_input[:], SILU)
+
+        table_rows = xT.rearrange("(a p i) t -> a i p t", p=P, i=PACK)
+        nc.sync.dma_start(tables[0, 0][:], table_rows[0, 0])
+        nc.sync.dma_start(gather_list[:], offs)
+        for first, picks in PIECE_PICKS.items():
+            nc.sync.dma_start(wgt_tiles[first][:], wgt[:, first : first + picks])
         for a in range(PASSES):
-            for t in range(PACK):
-                x[a, t] = keep.tile([P, TOKENS], F32, name=f"x{a}{t}")
-
-        nc.vector.memset(wsc[:].bitcast(I32), 0)
-        nc.gpsimd.memset(warm[:], 0.0)
-        for m in range(M_TILES):
-            nc.vector.memset(win[m][:], 0.0)
-        nc.scalar.activation(warm[:], warm[:], SILU)
-
-        planes = xT.rearrange("(a p t) n -> a t p n", p=P, t=PACK)
-        scale_rows = w_scales.rearrange("a (q r) n -> r q a n", r=PACK)
-
-        def load_x(a, t):
-            nc.sync.dma_start(x[a, t][:], planes[a, t])
-
-        def load_scales(r):
-            nc.sync.dma_start(
-                wsc[:].bitcast(I32)[r:P:32, :].rearrange("q (a n) -> q a n", a=PASSES),
-                scale_rows[r].bitcast(I32),
-            )
-
-        nc.sync.dma_start(offs_t[:], offs)
-        nc.sync.dma_start(wgt_t[0][:], wgt[:, 0:128])
-        load_x(0, 0)
-        nc.sync.dma_start(wgt_t[128][:], wgt[:, 128:512])
-        load_x(0, 1)
-        load_x(0, 2)
-        load_x(0, 3)
-        load_x(1, 0)
-        load_x(1, 1)
-        load_x(1, 2)
-        load_x(1, 3)
-        load_x(2, 0)
-        load_x(2, 1)
-        load_x(2, 2)
-        load_x(2, 3)
+            for i in range(PACK):
+                if (a, i) != (0, 0):
+                    nc.sync.dma_start(tables[a, i][:], table_rows[a, i])
         nc.sync.dma_start(
-            ww[:].rearrange("p (a n) -> p a n", a=PASSES),
+            weight_codes[:].rearrange("p (a n) -> p a n", a=PASSES),
             w_words.rearrange("a p n i -> p a (n i)").bitcast(I32),
         )
+        scale_rows = w_scales.rearrange("a (q r) n -> r q a n", r=PACK)
         for r in range(PACK):
-            load_scales(r)
+            nc.sync.dma_start(
+                weight_scales[:].bitcast(I32)[r:P:32, :].rearrange("q (a n) -> q a n", a=PASSES),
+                scale_rows[r].bitcast(I32),
+            )
         with nc.allow_non_contiguous_dma(reason="one bias value to a partition"):
             nc.sync.dma_start(bias[:], b.rearrange("(m p) -> p m", p=P))
-        nc.sync.dma_start(offs2_t[:], offs2)
-        nc.sync.dma_start(wgo_t[:], wgo)
+        nc.sync.dma_start(scatter_list[:], offs2)
+        nc.sync.dma_start(wgo_tile[:], wgo)
 
-        pieces = {0: 128, 128: 384}
-        qpieces = {0: [(0, 512)], 1: [(0, 256), (256, 256)], 2: [(0, 128), (128, 128), (256, 256)]}
-        g4 = {}
-        grouped = {}
-        codes = {}
-        scales = {}
+        grouped = [keep.tile([P, PICKS, PACK], BF16, name=f"grouped_{a}", align_bytes=64) for a in range(PASSES)]
+        codes = [keep.tile([P, PICKS], U32, name=f"codes_{a}", align_bytes=64) for a in range(PASSES)]
+        scales = [keep.tile([P, PICKS], U8, name=f"scales_{a}", align_bytes=64) for a in range(PASSES)]
+        gathered = {}
         for a in range(PASSES):
-            for s, n in pieces.items():
-                g4[a, s] = keep.tile([P, PACK, n], F32, name=f"g{a}_{s}")
-            for s, n in qpieces[a]:
-                grouped[a, s] = keep.tile([P, n, PACK], BF16, name=f"r{a}_{s}", align_bytes=64)
-            codes[a] = keep.tile([P, PICKS], U32, name=f"c{a}", align_bytes=64)
-            scales[a] = keep.tile([P, PICKS], U8, name=f"s{a}", align_bytes=64)
-        acc = {}
-        for m in range(M_TILES):
-            for h in range(2):
-                acc[m, h] = psum.tile([P, HALF], F32, name=f"acc{m}{h}")
+            gathered[a, WIDE] = keep.tile([P, PACK, PIECE_PICKS[WIDE]], F32, name=f"wide_{a}")[:]
+        narrow_0 = keep.tile([P, PACK, PIECE_PICKS[NARROW]], F32, name="narrow_0")
+        gathered[0, NARROW] = narrow_0[:]
+        sums = {
+            (m, h): psum.tile([P, HALF], F32, name=f"sum_{m}_{h}") for m in range(ROW_TILES) for h in range(2)
+        }
 
-        def gather(a, t, s):
-            n = pieces[s]
+        def gather(a, i, first):
+            picks = PIECE_PICKS[first]
+            piece_list = gather_list[:, first // LIST_STRIPE : (first + picks) // LIST_STRIPE]
             nc.vector.tensor_tensor(
-                g4[a, s][:, t, :],
-                x[a, t][:].indirect(offs_t[:, s // 16 : (s + n) // 16]),
-                wgt_t[s][:],
-                MULT,
+                gathered[a, first][:, i, :], tables[a, i][:].indirect(piece_list), wgt_tiles[first][:], MULT
             )
 
-        def interleave(a, s, n):
-            q0 = [q for q, w in qpieces[a] if q <= s < q + w][0]
-            g0 = 0 if s < 128 else 128
+        def interleave(a, start, stop):
+            first = WIDE if start >= WIDE else NARROW
             nc.scalar.copy(
-                grouped[a, q0][:, s - q0 : s - q0 + n, :],
-                g4[a, g0][:, :, s - g0 : s - g0 + n].rearrange("p t n -> p n t"),
+                grouped[a][:, start:stop, :],
+                gathered[a, first][:, :, start - first : stop - first].rearrange("p i j -> p j i"),
             )
 
-        def quantize(a, s):
-            n = dict(qpieces[a])[s]
+        def quantize(a, start, stop):
             nc.vector.quantize_mx(
-                out=codes[a][:, s : s + n].bitcast(FP8X4),
-                scales=scales[a][:, s : s + n],
-                in_=grouped[a, s][:].rearrange("p n t -> p (n t)"),
+                out=codes[a][:, start:stop].bitcast(FP8X4),
+                scales=scales[a][:, start:stop],
+                in_=grouped[a][:, start:stop, :].rearrange("p j i -> p (j i)"),
             )
 
         def multiply(a, h):
-            for m in range(M_TILES):
-                cols = slice(a * 256 + m * P, a * 256 + (m + 1) * P)
-                picks = slice(h * HALF, (h + 1) * HALF)
+            half_picks = slice(h * HALF, (h + 1) * HALF)
+            for m in range(ROW_TILES):
+                columns = slice(a * ROWS + m * P, a * ROWS + (m + 1) * P)
                 nc.tensor.matmul_mx(
-                    out=acc[m, h][:],
-                    lhsT=ww[:, cols].bitcast(FP8X4),
-                    lhsT_scale=wsc[:, cols],
-                    rhs=codes[a][:, picks].bitcast(FP8X4),
-                    rhs_scale=scales[a][:, picks],
+                    out=sums[m, h][:],
+                    lhsT=weight_codes[:, columns].bitcast(FP8X4),
+                    lhsT_scale=weight_scales[:, columns],
+                    rhs=codes[a][:, half_picks].bitcast(FP8X4),
+                    rhs_scale=scales[a][:, half_picks],
                     start=(a == 0),
                     stop=(a == PASSES - 1),
                 )
 
-        y = {}
+        activated = {}
 
-        def act(m, h):
-            y[m, h] = keep.tile([P, HALF], F32, name=f"y{m}{h}")
-            nc.scalar.activation(y[m, h][:], acc[m, h][:], SILU, bias=bias[:, m : m + 1])
+        def activate(h):
+            for m in range(ROW_TILES):
+                activated[m, h] = keep.tile([P, HALF], F32, name=f"activated_{m}_{h}")
+                nc.scalar.activation(activated[m, h][:], sums[m, h][:], SILU, bias=bias[:, m : m + 1])
 
         def scatter(m, h):
+            half_list = scatter_list[:, h * HALF // LIST_STRIPE : (h + 1) * HALF // LIST_STRIPE]
             nc.vector.tensor_tensor(
-                win[m][:].indirect(offs2_t[:, h * HCOLS : (h + 1) * HCOLS]),
-                y[m, h][:],
-                wgo_t[:, h * HALF : (h + 1) * HALF],
-                MULT,
+                windows[m][:].indirect(half_list), activated[m, h][:], wgo_tile[:, h * HALF : (h + 1) * HALF], MULT
             )
 
-        for t in range(PACK):
-            if t == 0:
-                gather(0, t, 0)
-            gather(0, t, 128)
-        interleave(0, 128, 384)
-        for t in range(PACK):
-            gather(1, t, 128)
-        for t in range(1, PACK):
-            gather(0, t, 0)
-        interleave(0, 0, 128)
-        interleave(1, 256, 256)
-        interleave(1, 128, 128)
-        for t in range(PACK):
-            gather(2, t, 128)
-            if t == 2:
-                quantize(0, 0)
-                multiply(0, 0)
-                multiply(0, 1)
-                quantize(1, 256)
-                multiply(1, 1)
-        interleave(2, 256, 256)
-        interleave(2, 128, 128)
-        for t in range(PACK):
-            gather(1, t, 0)
-        interleave(1, 0, 128)
-        quantize(2, 256)
+        for i in range(PACK):
+            gather(0, i, NARROW)
+            gather(0, i, WIDE)
+        interleave(0, NARROW, WIDE)
+        interleave(0, WIDE, PICKS)
+        for i in range(PACK):
+            gather(1, i, WIDE)
+        interleave(1, HALF, PICKS)
+        interleave(1, WIDE, HALF)
+        gather(2, 0, WIDE)
+        quantize(0, 0, PICKS)
+        multiply(0, 0)
+        multiply(0, 1)
+        gather(2, 1, WIDE)
+        gather(2, 2, WIDE)
+        quantize(1, HALF, PICKS)
+        multiply(1, 1)
+        gather(2, 3, WIDE)
+        interleave(2, HALF, PICKS)
+
+        narrow_late = keep.tile([P, 2 * PACK, PIECE_PICKS[NARROW]], F32, name="narrow_late", tag="wgt_wide")
+        gathered[1, NARROW] = narrow_late[:, 0:PACK, :]
+        gathered[2, NARROW] = narrow_late[:, PACK : 2 * PACK, :]
+        for i in range(PACK):
+            gather(1, i, NARROW)
+        interleave(2, WIDE, HALF)
+        interleave(1, NARROW, WIDE)
+        gather(2, 0, NARROW)
+        quantize(2, HALF, PICKS)
         multiply(2, 1)
-        act(0, 1)
-        act(1, 1)
-        for t in range(PACK):
-            gather(2, t, 0)
-        interleave(2, 0, 128)
-        quantize(2, 128)
-        quantize(1, 0)
+        activate(1)
+        for i in range(1, PACK):
+            gather(2, i, NARROW)
+        interleave(2, NARROW, WIDE)
+        quantize(1, 0, HALF)
         multiply(1, 0)
+
         scatter(0, 1)
-        quantize(2, 0)
+        quantize(2, 0, HALF)
         multiply(2, 0)
         scatter(1, 1)
-        act(0, 0)
-        act(1, 0)
-        scatter(0, 0)
-        nc.sync.dma_start(out[0:P, :], win[0][:])
-        scatter(1, 0)
-        nc.sync.dma_start(out[P : 2 * P, :], win[1][:])
+        activate(0)
+        for m in range(ROW_TILES):
+            scatter(m, 0)
+            nc.sync.dma_start(out[m * P : (m + 1) * P, :], windows[m][:])

from contextlib import ExitStack

import concourse.mybir as mybir

F32 = mybir.dt.float32
BF16 = mybir.dt.bfloat16
I32 = mybir.dt.int32
U32 = mybir.dt.uint32
U16 = mybir.dt.uint16
U8 = mybir.dt.uint8
FP8X4 = mybir.dt.float8_e4m3fn_x4
MULT = mybir.AluOpType.mult
SILU = mybir.ActivationFunctionType.Silu

P = 128
PACK = 4
K = 1536
PASSES = K // (P * PACK)
ROWS = 256
ROW_TILES = ROWS // P
TOKENS = 1024
PICKS = 512
HALF = PICKS // 2
LIST_STRIPE = 16

NARROW = 0
WIDE = 128
PIECE_PICKS = {NARROW: 128, WIDE: 384}

FLOPS = 2 * K * ROWS * PICKS


def tile_list_hboth_silu_kernel(tc, xT, w_words, w_scales, wgt, b, wgo, offs, offs2, out):
    nc = tc.nc
    with ExitStack() as ctx:
        lists = ctx.enter_context(tc.tile_pool(name="lists", bufs=1))
        keep = ctx.enter_context(tc.tile_pool(name="keep", bufs=1))
        psum = ctx.enter_context(tc.psum_pool(name="psum", bufs=1))

        gather_list = lists.tile([P, PICKS // LIST_STRIPE], U16, name="gather_list")
        scatter_list = lists.tile([P, PICKS // LIST_STRIPE], U16, name="scatter_list")
        weight_scales = keep.tile([P, PASSES * ROWS], U8, name="weight_scales", align_bytes=64)
        weight_codes = keep.tile([P, PASSES * ROWS], I32, name="weight_codes", align_bytes=64)
        bias = keep.tile([P, ROW_TILES], F32, name="bias")
        silu_input = keep.tile([P, 1], F32, name="silu_input")
        wgo_tile = keep.tile([P, PICKS], F32, name="wgo_tile")
        wgt_narrow = keep.tile([P, PIECE_PICKS[NARROW]], F32, name="wgt_narrow")
        wgt_wide = keep.tile([P, PIECE_PICKS[WIDE]], F32, name="wgt_wide", tag="wgt_wide")
        wgt_tiles = {NARROW: wgt_narrow, WIDE: wgt_wide}
        windows = [keep.tile([P, TOKENS], F32, name=f"window_{m}") for m in range(ROW_TILES)]
        tables = {
            (a, i): keep.tile([P, TOKENS], F32, name=f"table_{a}_{i}") for a in range(PASSES) for i in range(PACK)
        }

        nc.vector.memset(weight_scales[:].bitcast(I32), 0)
        for m in range(ROW_TILES):
            nc.vector.memset(windows[m][:], 0.0)
        nc.gpsimd.memset(silu_input[:], 0.0)
        nc.scalar.activation(silu_input[:], silu_input[:], SILU)

        table_rows = xT.rearrange("(a p i) t -> a i p t", p=P, i=PACK)
        nc.sync.dma_start(tables[0, 0][:], table_rows[0, 0])
        nc.sync.dma_start(gather_list[:], offs)
        for first, picks in PIECE_PICKS.items():
            nc.sync.dma_start(wgt_tiles[first][:], wgt[:, first : first + picks])
        for a in range(PASSES):
            for i in range(PACK):
                if (a, i) != (0, 0):
                    nc.sync.dma_start(tables[a, i][:], table_rows[a, i])
        nc.sync.dma_start(
            weight_codes[:].rearrange("p (a n) -> p a n", a=PASSES),
            w_words.rearrange("a p n i -> p a (n i)").bitcast(I32),
        )
        scale_rows = w_scales.rearrange("a (q r) n -> r q a n", r=PACK)
        for r in range(PACK):
            nc.sync.dma_start(
                weight_scales[:].bitcast(I32)[r:P:32, :].rearrange("q (a n) -> q a n", a=PASSES),
                scale_rows[r].bitcast(I32),
            )
        with nc.allow_non_contiguous_dma(reason="one bias value to a partition"):
            nc.sync.dma_start(bias[:], b.rearrange("(m p) -> p m", p=P))
        nc.sync.dma_start(scatter_list[:], offs2)
        nc.sync.dma_start(wgo_tile[:], wgo)

        grouped = [keep.tile([P, PICKS, PACK], BF16, name=f"grouped_{a}", align_bytes=64) for a in range(PASSES)]
        codes = [keep.tile([P, PICKS], U32, name=f"codes_{a}", align_bytes=64) for a in range(PASSES)]
        scales = [keep.tile([P, PICKS], U8, name=f"scales_{a}", align_bytes=64) for a in range(PASSES)]
        gathered = {}
        for a in range(PASSES):
            gathered[a, WIDE] = keep.tile([P, PACK, PIECE_PICKS[WIDE]], F32, name=f"wide_{a}")[:]
        narrow_0 = keep.tile([P, PACK, PIECE_PICKS[NARROW]], F32, name="narrow_0")
        gathered[0, NARROW] = narrow_0[:]
        sums = {
            (m, h): psum.tile([P, HALF], F32, name=f"sum_{m}_{h}") for m in range(ROW_TILES) for h in range(2)
        }

        def gather(a, i, first):
            picks = PIECE_PICKS[first]
            piece_list = gather_list[:, first // LIST_STRIPE : (first + picks) // LIST_STRIPE]
            nc.vector.tensor_tensor(
                gathered[a, first][:, i, :], tables[a, i][:].indirect(piece_list), wgt_tiles[first][:], MULT
            )

        def interleave(a, start, stop):
            first = WIDE if start >= WIDE else NARROW
            nc.scalar.copy(
                grouped[a][:, start:stop, :],
                gathered[a, first][:, :, start - first : stop - first].rearrange("p i j -> p j i"),
            )

        def quantize(a, start, stop):
            nc.vector.quantize_mx(
                out=codes[a][:, start:stop].bitcast(FP8X4),
                scales=scales[a][:, start:stop],
                in_=grouped[a][:, start:stop, :].rearrange("p j i -> p (j i)"),
            )

        def multiply(a, h):
            half_picks = slice(h * HALF, (h + 1) * HALF)
            for m in range(ROW_TILES):
                columns = slice(a * ROWS + m * P, a * ROWS + (m + 1) * P)
                nc.tensor.matmul_mx(
                    out=sums[m, h][:],
                    lhsT=weight_codes[:, columns].bitcast(FP8X4),
                    lhsT_scale=weight_scales[:, columns],
                    rhs=codes[a][:, half_picks].bitcast(FP8X4),
                    rhs_scale=scales[a][:, half_picks],
                    start=(a == 0),
                    stop=(a == PASSES - 1),
                )

        activated = {}

        def activate(h):
            for m in range(ROW_TILES):
                activated[m, h] = keep.tile([P, HALF], F32, name=f"activated_{m}_{h}")
                nc.scalar.activation(activated[m, h][:], sums[m, h][:], SILU, bias=bias[:, m : m + 1])

        def scatter(m, h):
            half_list = scatter_list[:, h * HALF // LIST_STRIPE : (h + 1) * HALF // LIST_STRIPE]
            nc.vector.tensor_tensor(
                windows[m][:].indirect(half_list), activated[m, h][:], wgo_tile[:, h * HALF : (h + 1) * HALF], MULT
            )

        for i in range(PACK):
            gather(0, i, NARROW)
            gather(0, i, WIDE)
        interleave(0, NARROW, WIDE)
        interleave(0, WIDE, PICKS)
        for i in range(PACK):
            gather(1, i, WIDE)
        interleave(1, HALF, PICKS)
        interleave(1, WIDE, HALF)
        gather(2, 0, WIDE)
        quantize(0, 0, PICKS)
        multiply(0, 0)
        multiply(0, 1)
        gather(2, 1, WIDE)
        gather(2, 2, WIDE)
        quantize(1, HALF, PICKS)
        multiply(1, 1)
        gather(2, 3, WIDE)
        interleave(2, HALF, PICKS)

        narrow_late = keep.tile([P, 2 * PACK, PIECE_PICKS[NARROW]], F32, name="narrow_late", tag="wgt_wide")
        gathered[1, NARROW] = narrow_late[:, 0:PACK, :]
        gathered[2, NARROW] = narrow_late[:, PACK : 2 * PACK, :]
        for i in range(PACK):
            gather(1, i, NARROW)
        interleave(2, WIDE, HALF)
        interleave(1, NARROW, WIDE)
        gather(2, 0, NARROW)
        quantize(2, HALF, PICKS)
        multiply(2, 1)
        activate(1)
        for i in range(1, PACK):
            gather(2, i, NARROW)
        interleave(2, NARROW, WIDE)
        quantize(1, 0, HALF)
        multiply(1, 0)

        scatter(0, 1)
        quantize(2, 0, HALF)
        multiply(2, 0)
        scatter(1, 1)
        activate(0)
        for m in range(ROW_TILES):
            scatter(m, 0)
            nc.sync.dma_start(out[m * P : (m + 1) * P, :], windows[m][:])
